import numpy as np
import ml_dtypes


def mxq(x, axis, fmt="e4m3"):
    dtype, down = {"e4m3": (ml_dtypes.float8_e4m3fn, 7), "e5m2": (ml_dtypes.float8_e5m2, 14)}[fmt]
    v = np.moveaxis(np.asarray(x, np.float32).astype(ml_dtypes.bfloat16).astype(np.float64), axis, -1)
    blocks = v.reshape(v.shape[:-1] + (-1, 32))
    amax = np.abs(blocks).max(-1, keepdims=True)
    byte = np.maximum(np.where(amax > 0, np.frexp(amax)[1] - 1 + 127, 0) - down, 1)
    scale = np.exp2(byte - 127.0)
    codes = (blocks / scale).astype(np.float32).astype(dtype).astype(np.float64)
    return np.moveaxis((codes * scale).reshape(v.shape), -1, axis)


WIDE = False


def mx_kscale(k, group=512):
    if not WIDE:
        return np.ones(k)
    levels = np.array([10, -10, 5, -5, 0])
    if group != 512:
        return np.exp2(np.random.permutation(np.resize(levels, k // group))).repeat(group)
    if k % 512:
        return np.exp2(np.random.permutation(np.resize(levels, k // 32))).repeat(32)
    a = np.empty((k // 512, 16))
    for p in range(k // 512):
        a[p, :8] = np.random.permutation(np.resize(levels, 8))
        for g in range(8):
            far = levels[np.abs(levels - a[p, g]) >= 10]
            a[p, g + 8] = far[np.random.randint(len(far))]
    return np.exp2(a.ravel()).repeat(32)


def f64(x):
    return np.asarray(x).astype(np.float64)


def striped(idx):
    return np.tile(np.asarray(idx).reshape(-1, 16).T, (8, 1)).astype(np.uint16)


def unstriped(offs):
    return offs[:16].T.reshape(-1).astype(np.int64)


H, KV, D, NQ, N = 2, 2, 256, 512, 512


def setup_inputs():
    n = np.random.standard_normal
    s = mx_kscale(D, 0)[:, None]
    u = mx_kscale(N)
    t = np.random.uniform(0.5, 2.0, N) * u
    v = n((KV, N, 128))
    return {
        "qT": (n((H, D, NQ)) * s * (0.70 / np.sqrt(D))).astype(np.float32),
        "kT": (n((KV, D, N)) / s).astype(np.float32),
        "t": t.reshape(N, 1).astype(np.float32),
        "v": (v / t[:, None]).astype(np.float32),
        "mask": (np.arange(N)[:, None] <= np.sort(np.random.randint(N // 4, N, NQ))[None, :]).astype(np.float32),
        "gn": np.tile(np.random.uniform(0.5, 2.0, 128), (128, 1)).astype(np.float32),
    }


def reference(qT, kT, t, v, mask, gn):
    a = mxq(f64(kT), 1, "e4m3").transpose(0, 2, 1) @ mxq(f64(qT), 1, "e4m3")
    p = np.maximum(a, 0.0)
    p = p * f64(mask)
    w = p * f64(t)
    y = mxq(w, 1, "e4m3").transpose(0, 2, 1) @ mxq(f64(v), 1, "e4m3")
    y = y / 16.0
    y = y / np.sqrt(np.mean(np.square(y), -1, keepdims=True) + 1e-5) * f64(gn)[:1]
    return y

@@ -1,0 +1,241 @@
+from contextlib import ExitStack
+
+import concourse.mybir as mybir
+
+F32 = mybir.dt.float32
+BF16 = mybir.dt.bfloat16
+U32 = mybir.dt.uint32
+U8 = mybir.dt.uint8
+FP8X4 = mybir.dt.float8_e4m3fn_x4
+ALU = mybir.AluOpType
+ACT = mybir.ActivationFunctionType
+
+H, D, NQ, N, E = 2, 256, 512, 512, 128
+P = 128
+PACK = 4
+ROWS = D // PACK
+QC = 128
+CHUNKS = NQ // QC
+LOADS = (256, 256)
+K_VECTOR = 84
+
+FLOPS = 2 * H * N * NQ * (D + E)
+
+
+def tile_rows_a_relu_mask_onorm_kernel(tc, qT, kT, t, v, mask, gn, out):
+    nc = tc.nc
+    with ExitStack() as ctx:
+        sb = ctx.enter_context(tc.tile_pool(name="sb", bufs=1))
+        ps = ctx.enter_context(tc.psum_pool(name="ps", bufs=1))
+        ctx.enter_context(tc.manual_schedule())
+
+        def sbuf(name, shape, dtype):
+            return sb.tile(shape, dtype, name=name, align_bytes=64)
+
+        k_raw = sbuf("k_raw", [P, PACK, N], F32)
+        t_sb = sbuf("t_sb", [P, PACK], F32)
+        q_raw = [sbuf("q_raw%d" % i, [P, PACK, n], F32) for i, n in enumerate(LOADS)]
+        m_raw = [sbuf("m_raw%d" % i, [P, PACK, n], F32) for i, n in enumerate(LOADS)]
+        starts = [sum(LOADS[:i]) for i in range(len(LOADS))]
+        v_raw = sbuf("v_raw", [P, H, PACK, E], F32)
+        gn_sb = sbuf("gn_sb", [P, E], F32)
+
+        q_hbm = qT.rearrange("h (p j) n -> (h p) j n", j=PACK)
+        m_hbm = mask.rearrange("(p r) n -> p r n", r=PACK)
+        nc.sync.dma_start(out=k_raw[:], in_=kT.rearrange("h (p j) n -> (h p) j n", j=PACK))
+        for i, n in enumerate(LOADS):
+            nc.sync.dma_start(out=q_raw[i][:], in_=q_hbm[:, :, starts[i]:starts[i] + n])
+            if i == 0:
+                nc.sync.dma_start(out=t_sb[:], in_=t.rearrange("(p r) o -> p (r o)", r=PACK))
+            if i == len(LOADS) - 1:
+                nc.sync.dma_start(out=v_raw[:], in_=v.rearrange("h (p j) e -> p h j e", j=PACK))
+            nc.sync.dma_start(out=m_raw[i][:], in_=m_hbm[:, :, starts[i]:starts[i] + n])
+        nc.sync.dma_start(out=gn_sb[:], in_=gn)
+
+        table = sbuf("table", [P, 2], F32)
+        nc.vector.memset(table[:, 0:1], 1.0)
+        nc.scalar.activation(out=table[:, 1:2], in_=table[:, 0:1], func=ACT.Abs_reciprocal_sqrt)
+
+        k_bf = sbuf("k_bf", [P, N * PACK], BF16)
+        k_codes = sbuf("k_codes", [P, N], U32)
+        k_scales = sbuf("k_scales", [P, N], U8)
+        v_bf = sbuf("v_bf", [P, H * E * PACK], BF16)
+        v_codes = sbuf("v_codes", [P, H * E], U32)
+        v_scales = sbuf("v_scales", [P, H * E], U8)
+        q_bf = [sbuf("q_bf%d" % c, [P, QC * PACK], BF16) for c in range(CHUNKS)]
+        q_codes = [sbuf("q_codes%d" % c, [P, QC], U32) for c in range(CHUNKS)]
+        q_scales = [sbuf("q_scales%d" % c, [P, QC], U8) for c in range(CHUNKS)]
+        mt_rows = [sbuf("mt_rows%d" % c, [P, PACK, QC], F32) for c in range(CHUNKS)]
+        mt = [sbuf("mt%d" % c, [P, QC * PACK], F32) for c in range(CHUNKS)]
+        w_bf = [sbuf("w_bf%d" % c, [P, H * QC * PACK], BF16) for c in range(CHUNKS)]
+        w_codes = [sbuf("w_codes%d" % c, [P, H * QC], U32) for c in range(CHUNKS)]
+        w_scales = [sbuf("w_scales%d" % c, [P, H * QC], U8) for c in range(CHUNKS)]
+        sumsq = sbuf("sumsq", [P, CHUNKS * H], F32)
+        rstd = sbuf("rstd", [P, CHUNKS * H], F32)
+        squares = sbuf("squares", [P, E], F32)
+        res = [sbuf("res%d" % c, [P, H, E], F32) for c in range(CHUNKS)]
+        scores = {}
+
+        def quantize(codes, scales, values):
+            nc.vector.quantize_mx(out=codes[:].bitcast(FP8X4), scales=scales[:], in_=values[:])
+
+        def vcopy(out, in_):
+            nc.vector.tensor_copy(out=out, in_=in_)
+
+        def scopy(out, in_):
+            nc.scalar.copy(out=out, in_=in_)
+
+        def pack_k(copy, s0, s1):
+            copy(k_bf[:].rearrange("p (r s j) -> p s j r", r=PACK, j=PACK)[:, s0:s1],
+                 k_raw[:].rearrange("p j (s r) -> p s j r", r=PACK)[:, s0:s1])
+
+        def cols(raw, c):
+            i = max(j for j in range(len(LOADS)) if starts[j] <= c * QC)
+            lo = c * QC - starts[i]
+            return raw[i][:, :, lo:lo + QC]
+
+        def pack_q(copy, c):
+            copy(q_bf[c][:].rearrange("p (a i j) -> p a j i", i=4, j=PACK),
+                 cols(q_raw, c).rearrange("p j (a i) -> p a j i", i=4))
+
+        def pack_v(copy):
+            copy(v_bf[:].rearrange("p (h a i j) -> p h a j i", h=H, i=4, j=PACK),
+                 v_raw[:].rearrange("p h j (a i) -> p h a j i", i=4))
+
+        def mask_t_vector(c):
+            nc.vector.tensor_tensor(
+                out=mt[c][:].rearrange("p (a i r) -> p a r i", i=4, r=PACK),
+                in0=cols(m_raw, c).rearrange("p r (a i) -> p a r i", i=4),
+                in1=t_sb[:].unsqueeze(1).unsqueeze(3).to_broadcast([P, QC // 4, PACK, 4]),
+                op=ALU.mult)
+
+        def mask_t_scalar(c):
+            for r in range(PACK):
+                nc.scalar.activation(out=mt_rows[c][:, r, :], in_=cols(m_raw, c)[:, r, :], func=ACT.Copy,
+                                     scale=t_sb[:, r:r + 1])
+            nc.scalar.copy(out=mt[c][:].rearrange("p (a i r) -> p a r i", i=4, r=PACK),
+                           in_=mt_rows[c][:].rearrange("p r (a i) -> p a r i", i=4))
+
+        def score(c, heads=range(H)):
+            for h in heads:
+                scores[c, h] = ps.tile([P, PACK, QC], F32, name="score%d" % h, tag="score%d" % h, bufs=2)
+                rows = slice(ROWS * h, ROWS * (h + 1))
+                for r in range(PACK):
+                    tok = slice(P * r, P * (r + 1))
+                    nc.tensor.matmul_mx(
+                        out=scores[c, h][:, r, :],
+                        lhsT=k_codes[rows, tok].bitcast(FP8X4), lhsT_scale=k_scales[rows, tok],
+                        rhs=q_codes[c][rows, :].bitcast(FP8X4), rhs_scale=q_scales[c][rows, :],
+                        start=True, stop=True)
+
+        def weigh(c, h):
+            nc.vector.scalar_tensor_tensor(
+                out=w_bf[c][:, h * QC * PACK:(h + 1) * QC * PACK].rearrange("p (n r) -> p n r", r=PACK),
+                in0=scores[c, h][:].rearrange("p r n -> p n r"), scalar=0.0,
+                in1=mt[c][:].rearrange("p (n r) -> p n r", r=PACK),
+                op0=ALU.max, op1=ALU.mult)
+
+        def quantize_w(c, h0=0, h1=H):
+            nc.vector.quantize_mx(out=w_codes[c][:, h0 * QC:h1 * QC].bitcast(FP8X4), scales=w_scales[c][:, h0 * QC:h1 * QC],
+                                  in_=w_bf[c][:, h0 * QC * PACK:h1 * QC * PACK])
+
+        y_bank = [ps.tile([P, 4, E], F32, name="y_bank%d" % b) for b in range(4)]
+        place = {(0, 0): (0, 0), (0, 1): (0, 1), (1, 0): (0, 2), (1, 1): (0, 3),
+                 (2, 0): (1, 0), (2, 1): (1, 1), (3, 0): (2, 0), (3, 1): (3, 0)}
+
+        def y(c, h):
+            bank, slot = place[c, h]
+            return y_bank[bank][:, slot, :]
+
+        def mix(c, heads=range(H)):
+            for h in heads:
+                feat = slice(E * h, E * (h + 1))
+                qs = slice(QC * h, QC * (h + 1))
+                nc.tensor.matmul_mx(
+                    out=y(c, h),
+                    lhsT=w_codes[c][:, qs].bitcast(FP8X4), lhsT_scale=w_scales[c][:, qs],
+                    rhs=v_codes[:, feat].bitcast(FP8X4), rhs_scale=v_scales[:, feat],
+                    start=True, stop=True)
+
+        def square(c, heads=range(H)):
+            for h in heads:
+                nc.scalar.activation(out=squares[:], in_=y(c, h), func=ACT.Square,
+                                     accum_out=sumsq[:, H * c + h:H * c + h + 1])
+
+        def root(lo, hi):
+            nc.scalar.activation(out=rstd[:, lo:hi], in_=sumsq[:, lo:hi], func=ACT.Abs_reciprocal_sqrt,
+                                 scale=1.0 / E, bias=256.0 * 1e-5)
+
+        def finish(c, heads=range(H)):
+            for h in heads:
+                nc.vector.scalar_tensor_tensor(
+                    out=res[c][:, h, :], in0=y(c, h), scalar=rstd[:, H * c + h:H * c + h + 1], in1=gn_sb[:],
+                    op0=ALU.mult, op1=ALU.mult)
+
+        def store(c, h0=0, h1=H):
+            nc.sync.dma_start(out=out[h0:h1, c * QC:(c + 1) * QC, :].rearrange("h q e -> q h e"),
+                              in_=res[c][:, h0:h1, :])
+
+        def quantize_q(c):
+            quantize(q_codes[c], q_scales[c], q_bf[c])
+
+        pack_k(vcopy, 0, K_VECTOR)
+        pack_k(scopy, K_VECTOR, P)
+        pack_q(scopy, 0)
+        quantize(k_codes, k_scales, k_bf)
+        quantize_q(0)
+        score(0)
+        mask_t_vector(0)
+        pack_q(scopy, 1)
+        quantize_q(1)
+        score(1)
+        mask_t_scalar(1)
+        pack_q(scopy, 2)
+        pack_q(scopy, 3)
+        pack_v(scopy)
+        mask_t_scalar(3)
+        weigh(0, 0)
+        weigh(0, 1)
+        weigh(1, 0)
+        quantize_q(2)
+        score(2, [0])
+        quantize_w(0)
+        weigh(1, 1)
+        score(2, [1])
+        mask_t_vector(2)
+        quantize_q(3)
+        quantize(v_codes, v_scales, v_bf)
+        weigh(2, 0)
+        score(3, [0])
+        quantize_w(1)
+        mix(0)
+        mix(1)
+        square(0)
+        square(1)
+        root(0, 4)
+        weigh(2, 1)
+        score(3, [1])
+        weigh(3, 0)
+        quantize_w(2)
+        mix(2)
+        square(2)
+        quantize_w(3, 0, 1)
+        mix(3, [0])
+        weigh(3, 1)
+        finish(0, [0])
+        quantize_w(3, 1, 2)
+        mix(3, [1])
+        square(3, [0])
+        root(4, 7)
+        square(3, [1])
+        root(7, 8)
+        finish(0, [1])
+        store(0)
+        finish(1)
+        store(1)
+        finish(2)
+        store(2)
+        finish(3, [0])
+        store(3, 0, 1)
+        finish(3, [1])
+        store(3, 1, 2)

@@ -42,11 +42,10 @@ def tile_rows_a_relu_mask_onorm_kernel(tc, qT, kT, t, v, mask, gn, out):
 
         q_hbm = qT.rearrange("h (p j) n -> (h p) j n", j=PACK)
         m_hbm = mask.rearrange("(p r) n -> p r n", r=PACK)
+        nc.scalar.dma_start(out=t_sb[:], in_=t.rearrange("(p r) o -> p (r o)", r=PACK))
         nc.sync.dma_start(out=k_raw[:], in_=kT.rearrange("h (p j) n -> (h p) j n", j=PACK))
         for i, n in enumerate(LOADS):
             nc.sync.dma_start(out=q_raw[i][:], in_=q_hbm[:, :, starts[i]:starts[i] + n])
-            if i == 0:
-                nc.sync.dma_start(out=t_sb[:], in_=t.rearrange("(p r) o -> p (r o)", r=PACK))
             if i == len(LOADS) - 1:
                 nc.sync.dma_start(out=v_raw[:], in_=v.rearrange("h (p j) e -> p h j e", j=PACK))
             nc.sync.dma_start(out=m_raw[i][:], in_=m_hbm[:, :, starts[i]:starts[i] + n])
@@ -86,8 +85,9 @@ def tile_rows_a_relu_mask_onorm_kernel(tc, qT, kT, t, v, mask, gn, out):
             nc.scalar.copy(out=out, in_=in_)
 
         def pack_k(copy, s0, s1):
-            copy(k_bf[:].rearrange("p (r s j) -> p s j r", r=PACK, j=PACK)[:, s0:s1],
-                 k_raw[:].rearrange("p j (s r) -> p s j r", r=PACK)[:, s0:s1])
+            for r0 in (0, 2):
+                copy(k_bf[:].rearrange("p (r s j) -> p s j r", r=PACK, j=PACK)[:, s0:s1, :, r0:r0 + 2],
+                     k_raw[:].rearrange("p j (s r) -> p s j r", r=PACK)[:, s0:s1, :, r0:r0 + 2])
 
         def cols(raw, c):
             i = max(j for j in range(len(LOADS)) if starts[j] <= c * QC)
@@ -95,26 +95,26 @@ def tile_rows_a_relu_mask_onorm_kernel(tc, qT, kT, t, v, mask, gn, out):
             return raw[i][:, :, lo:lo + QC]
 
         def pack_q(copy, c):
-            copy(q_bf[c][:].rearrange("p (a i j) -> p a j i", i=4, j=PACK),
-                 cols(q_raw, c).rearrange("p j (a i) -> p a j i", i=4))
+            copy(q_bf[c][:].rearrange("p (a i j) -> p a j i", i=2, j=PACK),
+                 cols(q_raw, c).rearrange("p j (a i) -> p a j i", i=2))
 
         def pack_v(copy):
-            copy(v_bf[:].rearrange("p (h a i j) -> p h a j i", h=H, i=4, j=PACK),
-                 v_raw[:].rearrange("p h j (a i) -> p h a j i", i=4))
+            copy(v_bf[:].rearrange("p (h a i j) -> p h a j i", h=H, i=2, j=PACK),
+                 v_raw[:].rearrange("p h j (a i) -> p h a j i", i=2))
 
         def mask_t_vector(c):
             nc.vector.tensor_tensor(
-                out=mt[c][:].rearrange("p (a i r) -> p a r i", i=4, r=PACK),
-                in0=cols(m_raw, c).rearrange("p r (a i) -> p a r i", i=4),
-                in1=t_sb[:].unsqueeze(1).unsqueeze(3).to_broadcast([P, QC // 4, PACK, 4]),
+                out=mt[c][:].rearrange("p (a i r) -> p a r i", i=2, r=PACK),
+                in0=cols(m_raw, c).rearrange("p r (a i) -> p a r i", i=2),
+                in1=t_sb[:].unsqueeze(1).unsqueeze(3).to_broadcast([P, QC // 2, PACK, 2]),
                 op=ALU.mult)
 
         def mask_t_scalar(c):
             for r in range(PACK):
                 nc.scalar.activation(out=mt_rows[c][:, r, :], in_=cols(m_raw, c)[:, r, :], func=ACT.Copy,
                                      scale=t_sb[:, r:r + 1])
-            nc.scalar.copy(out=mt[c][:].rearrange("p (a i r) -> p a r i", i=4, r=PACK),
-                           in_=mt_rows[c][:].rearrange("p r (a i) -> p a r i", i=4))
+            nc.scalar.copy(out=mt[c][:].rearrange("p (a i r) -> p a r i", i=2, r=PACK),
+                           in_=mt_rows[c][:].rearrange("p r (a i) -> p a r i", i=2))
 
         def score(c, heads=range(H)):
             for h in heads:
@@ -202,8 +202,8 @@ def tile_rows_a_relu_mask_onorm_kernel(tc, qT, kT, t, v, mask, gn, out):
         quantize_w(0)
         weigh(1, 1)
         score(2, [1])
-        mask_t_vector(2)
         quantize_q(3)
+        mask_t_vector(2)
         quantize(v_codes, v_scales, v_bf)
         weigh(2, 0)
         score(3, [0])

@@ -116,12 +116,13 @@ def tile_rows_a_relu_mask_onorm_kernel(tc, qT, kT, t, v, mask, gn, out):
             nc.scalar.copy(out=mt[c][:].rearrange("p (a i r) -> p a r i", i=2, r=PACK),
                            in_=mt_rows[c][:].rearrange("p r (a i) -> p a r i", i=2))
 
-        def score(c, heads=range(H)):
-            for h in heads:
+        def score(c):
+            for h in range(H):
                 scores[c, h] = ps.tile([P, PACK, QC], F32, name="score%d" % h, tag="score%d" % h, bufs=2)
-                rows = slice(ROWS * h, ROWS * (h + 1))
-                for r in range(PACK):
-                    tok = slice(P * r, P * (r + 1))
+            for r in range(PACK):
+                tok = slice(P * r, P * (r + 1))
+                for h in range(H):
+                    rows = slice(ROWS * h, ROWS * (h + 1))
                     nc.tensor.matmul_mx(
                         out=scores[c, h][:, r, :],
                         lhsT=k_codes[rows, tok].bitcast(FP8X4), lhsT_scale=k_scales[rows, tok],
@@ -198,23 +199,21 @@ def tile_rows_a_relu_mask_onorm_kernel(tc, qT, kT, t, v, mask, gn, out):
         weigh(0, 1)
         weigh(1, 0)
         quantize_q(2)
-        score(2, [0])
+        score(2)
         quantize_w(0)
         weigh(1, 1)
-        score(2, [1])
         quantize_q(3)
+        score(3)
+        quantize_w(1)
         mask_t_vector(2)
         quantize(v_codes, v_scales, v_bf)
-        weigh(2, 0)
-        score(3, [0])
-        quantize_w(1)
         mix(0)
         mix(1)
         square(0)
         square(1)
         root(0, 4)
+        weigh(2, 0)
         weigh(2, 1)
-        score(3, [1])
         weigh(3, 0)
         quantize_w(2)
         mix(2)

from contextlib import ExitStack

import concourse.mybir as mybir

F32 = mybir.dt.float32
BF16 = mybir.dt.bfloat16
U32 = mybir.dt.uint32
U8 = mybir.dt.uint8
FP8X4 = mybir.dt.float8_e4m3fn_x4
ALU = mybir.AluOpType
ACT = mybir.ActivationFunctionType

H, D, NQ, N, E = 2, 256, 512, 512, 128
P = 128
PACK = 4
ROWS = D // PACK
QC = 128
CHUNKS = NQ // QC
LOADS = (256, 256)
K_VECTOR = 84

FLOPS = 2 * H * N * NQ * (D + E)


def tile_rows_a_relu_mask_onorm_kernel(tc, qT, kT, t, v, mask, gn, out):
    nc = tc.nc
    with ExitStack() as ctx:
        sb = ctx.enter_context(tc.tile_pool(name="sb", bufs=1))
        ps = ctx.enter_context(tc.psum_pool(name="ps", bufs=1))
        ctx.enter_context(tc.manual_schedule())

        def sbuf(name, shape, dtype):
            return sb.tile(shape, dtype, name=name, align_bytes=64)

        k_raw = sbuf("k_raw", [P, PACK, N], F32)
        t_sb = sbuf("t_sb", [P, PACK], F32)
        q_raw = [sbuf("q_raw%d" % i, [P, PACK, n], F32) for i, n in enumerate(LOADS)]
        m_raw = [sbuf("m_raw%d" % i, [P, PACK, n], F32) for i, n in enumerate(LOADS)]
        starts = [sum(LOADS[:i]) for i in range(len(LOADS))]
        v_raw = sbuf("v_raw", [P, H, PACK, E], F32)
        gn_sb = sbuf("gn_sb", [P, E], F32)

        q_hbm = qT.rearrange("h (p j) n -> (h p) j n", j=PACK)
        m_hbm = mask.rearrange("(p r) n -> p r n", r=PACK)
        nc.scalar.dma_start(out=t_sb[:], in_=t.rearrange("(p r) o -> p (r o)", r=PACK))
        nc.sync.dma_start(out=k_raw[:], in_=kT.rearrange("h (p j) n -> (h p) j n", j=PACK))
        for i, n in enumerate(LOADS):
            nc.sync.dma_start(out=q_raw[i][:], in_=q_hbm[:, :, starts[i]:starts[i] + n])
            if i == len(LOADS) - 1:
                nc.sync.dma_start(out=v_raw[:], in_=v.rearrange("h (p j) e -> p h j e", j=PACK))
            nc.sync.dma_start(out=m_raw[i][:], in_=m_hbm[:, :, starts[i]:starts[i] + n])
        nc.sync.dma_start(out=gn_sb[:], in_=gn)

        table = sbuf("table", [P, 2], F32)
        nc.vector.memset(table[:, 0:1], 1.0)
        nc.scalar.activation(out=table[:, 1:2], in_=table[:, 0:1], func=ACT.Abs_reciprocal_sqrt)

        k_bf = sbuf("k_bf", [P, N * PACK], BF16)
        k_codes = sbuf("k_codes", [P, N], U32)
        k_scales = sbuf("k_scales", [P, N], U8)
        v_bf = sbuf("v_bf", [P, H * E * PACK], BF16)
        v_codes = sbuf("v_codes", [P, H * E], U32)
        v_scales = sbuf("v_scales", [P, H * E], U8)
        q_bf = [sbuf("q_bf%d" % c, [P, QC * PACK], BF16) for c in range(CHUNKS)]
        q_codes = [sbuf("q_codes%d" % c, [P, QC], U32) for c in range(CHUNKS)]
        q_scales = [sbuf("q_scales%d" % c, [P, QC], U8) for c in range(CHUNKS)]
        mt_rows = [sbuf("mt_rows%d" % c, [P, PACK, QC], F32) for c in range(CHUNKS)]
        mt = [sbuf("mt%d" % c, [P, QC * PACK], F32) for c in range(CHUNKS)]
        w_bf = [sbuf("w_bf%d" % c, [P, H * QC * PACK], BF16) for c in range(CHUNKS)]
        w_codes = [sbuf("w_codes%d" % c, [P, H * QC], U32) for c in range(CHUNKS)]
        w_scales = [sbuf("w_scales%d" % c, [P, H * QC], U8) for c in range(CHUNKS)]
        sumsq = sbuf("sumsq", [P, CHUNKS * H], F32)
        rstd = sbuf("rstd", [P, CHUNKS * H], F32)
        squares = sbuf("squares", [P, E], F32)
        res = [sbuf("res%d" % c, [P, H, E], F32) for c in range(CHUNKS)]
        scores = {}

        def quantize(codes, scales, values):
            nc.vector.quantize_mx(out=codes[:].bitcast(FP8X4), scales=scales[:], in_=values[:])

        def vcopy(out, in_):
            nc.vector.tensor_copy(out=out, in_=in_)

        def scopy(out, in_):
            nc.scalar.copy(out=out, in_=in_)

        def pack_k(copy, s0, s1):
            for r0 in (0, 2):
                copy(k_bf[:].rearrange("p (r s j) -> p s j r", r=PACK, j=PACK)[:, s0:s1, :, r0:r0 + 2],
                     k_raw[:].rearrange("p j (s r) -> p s j r", r=PACK)[:, s0:s1, :, r0:r0 + 2])

        def cols(raw, c):
            i = max(j for j in range(len(LOADS)) if starts[j] <= c * QC)
            lo = c * QC - starts[i]
            return raw[i][:, :, lo:lo + QC]

        def pack_q(copy, c):
            copy(q_bf[c][:].rearrange("p (a i j) -> p a j i", i=2, j=PACK),
                 cols(q_raw, c).rearrange("p j (a i) -> p a j i", i=2))

        def pack_v(copy):
            copy(v_bf[:].rearrange("p (h a i j) -> p h a j i", h=H, i=2, j=PACK),
                 v_raw[:].rearrange("p h j (a i) -> p h a j i", i=2))

        def mask_t_vector(c):
            nc.vector.tensor_tensor(
                out=mt[c][:].rearrange("p (a i r) -> p a r i", i=2, r=PACK),
                in0=cols(m_raw, c).rearrange("p r (a i) -> p a r i", i=2),
                in1=t_sb[:].unsqueeze(1).unsqueeze(3).to_broadcast([P, QC // 2, PACK, 2]),
                op=ALU.mult)

        def mask_t_scalar(c):
            for r in range(PACK):
                nc.scalar.activation(out=mt_rows[c][:, r, :], in_=cols(m_raw, c)[:, r, :], func=ACT.Copy,
                                     scale=t_sb[:, r:r + 1])
            nc.scalar.copy(out=mt[c][:].rearrange("p (a i r) -> p a r i", i=2, r=PACK),
                           in_=mt_rows[c][:].rearrange("p r (a i) -> p a r i", i=2))

        def score(c):
            for h in range(H):
                scores[c, h] = ps.tile([P, PACK, QC], F32, name="score%d" % h, tag="score%d" % h, bufs=2)
            for r in range(PACK):
                tok = slice(P * r, P * (r + 1))
                for h in range(H):
                    rows = slice(ROWS * h, ROWS * (h + 1))
                    nc.tensor.matmul_mx(
                        out=scores[c, h][:, r, :],
                        lhsT=k_codes[rows, tok].bitcast(FP8X4), lhsT_scale=k_scales[rows, tok],
                        rhs=q_codes[c][rows, :].bitcast(FP8X4), rhs_scale=q_scales[c][rows, :],
                        start=True, stop=True)

        def weigh(c, h):
            nc.vector.scalar_tensor_tensor(
                out=w_bf[c][:, h * QC * PACK:(h + 1) * QC * PACK].rearrange("p (n r) -> p n r", r=PACK),
                in0=scores[c, h][:].rearrange("p r n -> p n r"), scalar=0.0,
                in1=mt[c][:].rearrange("p (n r) -> p n r", r=PACK),
                op0=ALU.max, op1=ALU.mult)

        def quantize_w(c, h0=0, h1=H):
            nc.vector.quantize_mx(out=w_codes[c][:, h0 * QC:h1 * QC].bitcast(FP8X4), scales=w_scales[c][:, h0 * QC:h1 * QC],
                                  in_=w_bf[c][:, h0 * QC * PACK:h1 * QC * PACK])

        y_bank = [ps.tile([P, 4, E], F32, name="y_bank%d" % b) for b in range(4)]
        place = {(0, 0): (0, 0), (0, 1): (0, 1), (1, 0): (0, 2), (1, 1): (0, 3),
                 (2, 0): (1, 0), (2, 1): (1, 1), (3, 0): (2, 0), (3, 1): (3, 0)}

        def y(c, h):
            bank, slot = place[c, h]
            return y_bank[bank][:, slot, :]

        def mix(c, heads=range(H)):
            for h in heads:
                feat = slice(E * h, E * (h + 1))
                qs = slice(QC * h, QC * (h + 1))
                nc.tensor.matmul_mx(
                    out=y(c, h),
                    lhsT=w_codes[c][:, qs].bitcast(FP8X4), lhsT_scale=w_scales[c][:, qs],
                    rhs=v_codes[:, feat].bitcast(FP8X4), rhs_scale=v_scales[:, feat],
                    start=True, stop=True)

        def square(c, heads=range(H)):
            for h in heads:
                nc.scalar.activation(out=squares[:], in_=y(c, h), func=ACT.Square,
                                     accum_out=sumsq[:, H * c + h:H * c + h + 1])

        def root(lo, hi):
            nc.scalar.activation(out=rstd[:, lo:hi], in_=sumsq[:, lo:hi], func=ACT.Abs_reciprocal_sqrt,
                                 scale=1.0 / E, bias=256.0 * 1e-5)

        def finish(c, heads=range(H)):
            for h in heads:
                nc.vector.scalar_tensor_tensor(
                    out=res[c][:, h, :], in0=y(c, h), scalar=rstd[:, H * c + h:H * c + h + 1], in1=gn_sb[:],
                    op0=ALU.mult, op1=ALU.mult)

        def store(c, h0=0, h1=H):
            nc.sync.dma_start(out=out[h0:h1, c * QC:(c + 1) * QC, :].rearrange("h q e -> q h e"),
                              in_=res[c][:, h0:h1, :])

        def quantize_q(c):
            quantize(q_codes[c], q_scales[c], q_bf[c])

        pack_k(vcopy, 0, K_VECTOR)
        pack_k(scopy, K_VECTOR, P)
        pack_q(scopy, 0)
        quantize(k_codes, k_scales, k_bf)
        quantize_q(0)
        score(0)
        mask_t_vector(0)
        pack_q(scopy, 1)
        quantize_q(1)
        score(1)
        mask_t_scalar(1)
        pack_q(scopy, 2)
        pack_q(scopy, 3)
        pack_v(scopy)
        mask_t_scalar(3)
        weigh(0, 0)
        weigh(0, 1)
        weigh(1, 0)
        quantize_q(2)
        score(2)
        quantize_w(0)
        weigh(1, 1)
        quantize_q(3)
        score(3)
        quantize_w(1)
        mask_t_vector(2)
        quantize(v_codes, v_scales, v_bf)
        mix(0)
        mix(1)
        square(0)
        square(1)
        root(0, 4)
        weigh(2, 0)
        weigh(2, 1)
        weigh(3, 0)
        quantize_w(2)
        mix(2)
        square(2)
        quantize_w(3, 0, 1)
        mix(3, [0])
        weigh(3, 1)
        finish(0, [0])
        quantize_w(3, 1, 2)
        mix(3, [1])
        square(3, [0])
        root(4, 7)
        square(3, [1])
        root(7, 8)
        finish(0, [1])
        store(0)
        finish(1)
        store(1)
        finish(2)
        store(2)
        finish(3, [0])
        store(3, 0, 1)
        finish(3, [1])
        store(3, 1, 2)
